import numpy as np
import ml_dtypes


def mxq(x, axis, fmt="e4m3"):
    dtype, down = {"e4m3": (ml_dtypes.float8_e4m3fn, 7), "e5m2": (ml_dtypes.float8_e5m2, 14)}[fmt]
    v = np.moveaxis(np.asarray(x, np.float32).astype(ml_dtypes.bfloat16).astype(np.float64), axis, -1)
    blocks = v.reshape(v.shape[:-1] + (-1, 32))
    amax = np.abs(blocks).max(-1, keepdims=True)
    byte = np.maximum(np.where(amax > 0, np.frexp(amax)[1] - 1 + 127, 0) - down, 1)
    scale = np.exp2(byte - 127.0)
    codes = (blocks / scale).astype(np.float32).astype(dtype).astype(np.float64)
    return np.moveaxis((codes * scale).reshape(v.shape), -1, axis)


WIDE = False


def mx_kscale(k):
    if not WIDE:
        return np.ones(k)
    levels = np.array([10, -10, 5, -5, 0])
    if k % 512:
        return np.exp2(np.random.permutation(np.resize(levels, k // 32))).repeat(32)
    a = np.empty((k // 512, 16))
    for p in range(k // 512):
        a[p, :8] = np.random.permutation(np.resize(levels, 8))
        for g in range(8):
            far = levels[np.abs(levels - a[p, g]) >= 10]
            a[p, g + 8] = far[np.random.randint(len(far))]
    return np.exp2(a.ravel()).repeat(32)


def f64(x):
    return np.asarray(x).astype(np.float64)


def striped(idx):
    return np.tile(idx.reshape(-1, 16).T, (8, 1)).astype(np.uint16)


def unstriped(offs):
    return offs[:16].T.reshape(-1).astype(np.int64)


E2M1 = np.array([0.0, 0.5, 1.0, 1.5, 2.0, 3.0, 4.0, 6.0, -0.0, -0.5, -1.0, -1.5, -2.0, -3.0, -4.0, -6.0])


def pack_weight(w, fmt):
    k, n = w.shape
    w = f64(np.asarray(w, np.float32).astype(ml_dtypes.bfloat16)).reshape(k // 32, 32, n)
    amax = np.abs(w).max(1)
    if fmt == "e4m3":
        byte = np.frexp(amax)[1] - 1 + 127 - 7
    else:
        mant, ex = np.frexp(amax / 6.0)
        byte = np.where(mant > 0.5, ex, ex - 1) + 127
    byte = np.clip(np.where(amax > 0, byte, 1), 1, 254)
    scaled = (w * np.exp2(127.0 - byte)[:, None, :]).reshape(k, n).astype(np.float32)
    by_word = np.ascontiguousarray(scaled.reshape(k // 512, 128, 4, n).transpose(0, 1, 3, 2))
    if fmt == "e4m3":
        words = by_word.astype(ml_dtypes.float8_e4m3fn).view(np.uint8)
    else:
        c = by_word.astype(ml_dtypes.float4_e2m1fn).view(np.uint8) & 0xF
        words = (c[..., 0::2] | (c[..., 1::2] << 4)).reshape(k // 512, 128, 2 * n)
    return np.ascontiguousarray(words), np.ascontiguousarray(byte.astype(np.uint8).reshape(k // 512, 16, n))


def unpack_weight(words, scales, fmt):
    g, _, n = scales.shape
    words = np.ascontiguousarray(words).reshape(g, 128, n, -1)
    if fmt == "e4m3":
        vals = words.view(ml_dtypes.float8_e4m3fn).astype(np.float64)
    else:
        nib = np.empty((g, 128, n, 4), np.uint8)
        nib[..., 0::2] = words & 0xF
        nib[..., 1::2] = words >> 4
        vals = E2M1[nib]
    vals = vals * np.repeat(np.exp2(scales.astype(np.float64) - 127.0), 8, axis=1)[..., None]
    return vals.transpose(0, 1, 3, 2).reshape(g * 512, n)


def gelu(v):
    return 0.5 * v * (1.0 + np.tanh(np.sqrt(2.0 / np.pi) * (v + 0.044715 * v**3)))


def striped8(idx):
    return np.concatenate([v.reshape(-1, 16).T for v in idx]).astype(np.uint16)


def unstriped8(offs):
    return np.stack([offs[16 * g:16 * g + 16].T.reshape(-1) for g in range(8)]).astype(np.int64)


def heads(h, wgt, idx8):
    r = np.arange(h.shape[0])
    return wgt[r // 4 % 128] * h[r[:, None], idx8[r % 512 // 64]]


def put_heads(h, wgs, idx8, t2):
    r = np.arange(h.shape[0])
    page = np.zeros((h.shape[0], t2))
    page[r[:, None], idx8[r % 512 // 64]] = wgs[r // 4 % 128] * h
    return page


K, H, N, T, S, P, T2 = 1024, 1024, 512, 4096, 1024, 512, 1024


def setup_inputs():
    n = np.random.standard_normal
    s = mx_kscale(K)[:, None]
    u = mx_kscale(H)[:, None]
    d = {}
    d["tab_words"], d["tab_scales"] = pack_weight(n((K, T)) * s, "e4m3")
    d["offs"] = striped(np.random.permutation(T)[:S])
    d["w1_words"], d["w1_scales"] = pack_weight(n((K, H)) / s * u.T / K ** 0.5, "e2m1")
    d["offs2"] = striped8(np.stack([np.random.permutation(S)[:P] for _ in range(8)]))
    d["wgt"] = np.repeat(np.random.uniform(0.5, 2.0, (8, P)), 16, axis=0).astype(np.float32)
    d["target"] = (n(H) * u[:, 0]).astype(np.float32)
    d["w2"] = (n((H, N)) / u / H ** 0.5).astype(np.float32)
    d["w3_words"], d["w3_scales"] = pack_weight(n((H, N)) / u / H ** 0.5, "e4m3")
    d["offs3"] = striped8(np.stack([np.random.permutation(T2)[:P] for _ in range(8)]))
    d["wgo"] = np.repeat(np.random.uniform(0.5, 2.0, (8, P)), 16, axis=0).astype(np.float32)
    return d


def reference(tab_words, tab_scales, offs, w1_words, w1_scales, offs2, wgt, target, w2, w3_words, w3_scales, offs3, wgo):
    v = unpack_weight(tab_words, tab_scales, "e4m3")[:, unstriped(offs)]
    w1 = unpack_weight(w1_words, w1_scales, "e2m1")
    w3 = unpack_weight(w3_words, w3_scales, "e4m3")
    h = w1.T @ v
    x = heads(h, f64(wgt), unstriped8(offs2))
    shifted = x + f64(target)[:, None]
    bare = np.abs(x)
    ya = mxq(f64(w2), 0, "e4m3").T @ mxq(shifted, 0, "e4m3")
    yb = w3.T @ mxq(bare, 0, "e4m3")
    dev = ya - yb
    y = np.log(np.square(dev) + 1.0)
    out = put_heads(y, f64(wgo), unstriped8(offs3), T2)
    return out

@@ -1,0 +1,262 @@
+from contextlib import ExitStack
+
+import concourse.mybir as mybir
+
+K, H, N, T, S, PICK, T2 = 1024, 1024, 512, 4096, 1024, 512, 1024
+FLOPS = 2 * K * H * S + 2 * 2 * H * N * PICK
+
+F32 = mybir.dt.float32
+BF16 = mybir.dt.bfloat16
+I32 = mybir.dt.int32
+U32 = mybir.dt.uint32
+U16 = mybir.dt.uint16
+U8 = mybir.dt.uint8
+FP8X4 = mybir.dt.float8_e4m3fn_x4
+FP4X4 = mybir.dt.float4_e2m1fn_x4
+ACT = mybir.ActivationFunctionType
+ALU = mybir.AluOpType
+
+P = 128
+PACK = 4
+KP = P * PACK
+BANK = 512
+
+
+def tile_list_pod_cure_deviation_kernel(
+    tc, tab_words, tab_scales, offs, w1_words, w1_scales, offs2, wgt, target, w2, w3_words, w3_scales, offs3, wgo, out
+):
+    nc = tc.nc
+    with ExitStack() as ctx:
+        keep = ctx.enter_context(tc.tile_pool(name="keep", bufs=1))
+        psum = ctx.enter_context(tc.psum_pool(name="psum", bufs=8))
+
+        def sb(shape, dtype, name, tag=""):
+            return keep.tile(shape, dtype, name=name, tag=tag or name, align_bytes=64)
+
+        list1 = sb([P, S // 16], U16, "list1")
+        list2 = sb([P, PICK // 16], U16, "list2")
+        list3 = sb([P, PICK // 16], U16, "list3")
+        tab_sc = sb([P, T], U8, "tab_sc")
+        v_sc0 = sb([P, S], U8, "v_sc0")
+        v_sc1 = sb([P, S], U8, "v_sc1")
+        w1_raw = [sb([P, 2 * H], U8, f"w1_raw{b}") for b in range(2)]
+        w1_sc_raw = sb([P, 2 * H], U8, "w1_sc_raw")
+        w3_sc_raw = sb([P, N], U8, "w3_sc_raw")
+        pages = [sb([P, T2], F32, f"page{i}") for i in range(PACK)]
+        warm = sb([P, 1], F32, "warm")
+        warm_out = sb([P, 1], F32, "warm_out")
+
+        nc.vector.memset(tab_sc[:].bitcast(I32), 0)
+        nc.vector.memset(w1_sc_raw[:].bitcast(I32), 0)
+        nc.vector.memset(warm[:], 1.0)
+        nc.vector.memset(v_sc1[:].bitcast(I32), 0)
+        for i in range(PACK):
+            nc.vector.memset(pages[i][:], 0.0)
+        nc.vector.memset(w3_sc_raw[:].bitcast(I32), 0)
+
+        tab = [sb([P, T], I32, f"tab{a}") for a in range(2)]
+
+        def load_w1(b):
+            nc.sync.dma_start(
+                w1_raw[b][:].bitcast(I32).rearrange("p (a c) -> p a c", a=2),
+                w1_words[:, :, b * H : (b + 1) * H].bitcast(I32).rearrange("a p c -> p a c"),
+            )
+
+        nc.sync.dma_start(list1[:], offs)
+        nc.sync.dma_start(tab[0][:], tab_words[0].rearrange("p t i -> p (t i)").bitcast(I32))
+        for q in range(4):
+            nc.scalar.dma_start(
+                tab_sc[32 * q : 32 * q + 8, :].bitcast(I32), tab_scales[:, 4 * q : 4 * q + 4, :].bitcast(I32)
+            )
+        for q in range(4):
+            nc.scalar.dma_start(
+                w1_sc_raw[32 * q : 32 * q + 4, :].bitcast(I32).rearrange("r (a c) -> r a c", a=2),
+                w1_scales[:, 4 * q : 4 * q + 4, :].bitcast(I32).rearrange("a r c -> r a c"),
+            )
+        load_w1(0)
+        nc.sync.dma_start(tab[1][:], tab_words[1].rearrange("p t i -> p (t i)").bitcast(I32))
+        nc.scalar.activation(warm_out[:], warm[:], ACT.Ln)
+
+        nc.vector.tensor_copy(v_sc0[:], tab_sc[:].indirect(list1[:]))
+        nc.scalar.dma_start(v_sc1[0 : P - 4, :].bitcast(I32), v_sc0[4:P, :].bitcast(I32))
+        v_sc = [v_sc0, v_sc1]
+
+        load_w1(1)
+        nc.sync.dma_start(list2[:], offs2)
+        wgt_sb = sb([P, PICK], F32, "wgt_sb")
+        nc.sync.dma_start(wgt_sb[:], wgt)
+        tgt = sb([P, 2, PACK], F32, "tgt")
+        nc.sync.dma_start(tgt[:], target.rearrange("(b p t) -> p b t", b=2, t=PACK))
+        w2_raw = []
+        for a in range(2):
+            raw = sb([P, PACK * N], F32, f"w2_raw{a}")
+            nc.sync.dma_start(raw[:], w2[a * KP : (a + 1) * KP, :].rearrange("(p j) n -> p (j n)", j=PACK))
+            w2_raw.append(raw)
+        w3_raw = sb([P, 2 * N], I32, "w3_raw")
+        nc.sync.dma_start(
+            w3_raw[:].rearrange("p (a c) -> p a c", a=2),
+            w3_words.rearrange("a p c i -> p a (c i)").bitcast(I32),
+        )
+        for q in range(4):
+            nc.sync.dma_start(
+                w3_sc_raw[32 * q : 32 * q + 8, :].bitcast(I32), w3_scales[:, 4 * q : 4 * q + 4, :].bitcast(I32)
+            )
+        nc.sync.dma_start(list3[:], offs3)
+        wgo_sb = sb([P, PICK], F32, "wgo_sb")
+        nc.sync.dma_start(wgo_sb[:], wgo)
+
+        def deal_w1(b, tag):
+            dealt = sb([P, 3 * H], U8, f"w1_dealt{b}", tag)
+            nc.vector.tensor_copy(
+                dealt[:, 0 : 2 * H].bitcast(U16).rearrange("p (a t m) -> p a t m", t=PACK, m=P),
+                w1_raw[b][:].bitcast(U16).rearrange("p (a m t) -> p a t m", t=PACK, m=P),
+            )
+            nc.vector.tensor_copy(
+                dealt[:, 2 * H : 3 * H].rearrange("p (a t m) -> p a t m", t=PACK, m=P),
+                w1_sc_raw[:].rearrange("p (a b m t) -> p b a t m", a=2, t=PACK, m=P)[:, b],
+            )
+            return dealt
+
+        v = [sb([P, S], U32, f"v{a}") for a in range(2)]
+        nc.vector.tensor_copy(v[0][:], tab[0][:].bitcast(U32).indirect(list1[:]))
+        w1 = [deal_w1(0, "")]
+        for j in range(2):
+            nc.vector.tensor_copy(
+                v[1][:, j * BANK : (j + 1) * BANK], tab[1][:].bitcast(U32).indirect(list1[:, 32 * j : 32 * (j + 1)])
+            )
+        w1.append(deal_w1(1, "tab1"))
+
+        def stage1_pass(bank, a, b, t, j):
+            c0 = a * KP + t * P
+            cols = slice(j * BANK, (j + 1) * BANK)
+            nc.tensor.matmul_mx(
+                out=bank[:],
+                lhsT=w1[b][:, 2 * c0 : 2 * (c0 + P)].bitcast(FP4X4),
+                lhsT_scale=w1[b][:, 2 * H + c0 : 2 * H + c0 + P],
+                rhs=v[a][:, cols].bitcast(FP8X4),
+                rhs_scale=v_sc[a][:, cols],
+                start=(a == 0),
+                stop=(a == 1),
+            )
+
+        x = [sb([P, PACK, PICK], F32, f"x{b}") for b in range(2)]
+
+        def pick(banks, b, t):
+            h = sb([P, S], F32, f"h{b}{t}")
+            for j in range(2):
+                nc.scalar.copy(h[:, j * BANK : (j + 1) * BANK], banks[j][:])
+            nc.vector.tensor_tensor(x[b][:, t, :], h[:].indirect(list2[:]), wgt_sb[:], ALU.mult)
+
+        def quantise(src, name, tag=""):
+            codes = sb([P, src.shape[1] // PACK], U32, name + "_c", tag)
+            plane = sb([P, src.shape[1] // PACK], U8, name + "_s")
+            nc.vector.quantize_mx(out=codes[:].bitcast(FP8X4), scales=plane[:], in_=src)
+            return codes, plane
+
+        def woven(tile):
+            return tile[:].rearrange("p (c i t) -> p c t i", i=4, t=PACK)
+
+        def rows(b):
+            return x[b][:].rearrange("p t (c i) -> p c t i", i=4)
+
+        def magnitudes(b):
+            mag = sb([P, PACK * PICK], BF16, f"mag{b}")
+            nc.scalar.activation(woven(mag), rows(b), ACT.Abs)
+            return mag
+
+        def shifted(b):
+            sh = sb([P, PACK * PICK], BF16, f"sh{b}")
+            nc.vector.tensor_tensor(
+                woven(sh), rows(b), tgt[:, b, :].unsqueeze(1).unsqueeze(3).to_broadcast([P, PICK // 4, PACK, 4]), ALU.add
+            )
+            return sh
+
+        first = [[psum.tile([P, BANK], F32, name="bank") for j in range(2)] for t in range(PACK)]
+        for t in range(PACK):
+            for j in range(2):
+                stage1_pass(first[t][j], 0, 0, t, j)
+        for j in range(2):
+            for t in range(PACK):
+                stage1_pass(first[t][j], 1, 0, t, j)
+        for t in range(PACK):
+            pick(first[t], 0, t)
+        for t in range(PACK):
+            banks = [psum.tile([P, BANK], F32, name="bank") for j in range(2)]
+            for j in range(2):
+                for a in range(2):
+                    stage1_pass(banks[j], a, 1, t, j)
+            pick(banks, 1, t)
+
+        w3_sc = sb([P, N], U8, "w3_sc")
+        nc.vector.tensor_copy(
+            w3_sc[:].rearrange("p (t m) -> p t m", t=PACK),
+            w3_sc_raw[:].rearrange("p (m t) -> p t m", t=PACK),
+        )
+        w3_by_slice = w3_raw[:].rearrange("p (x t) -> p x t", t=PACK)
+        w3_first = sb([P, 2 * P], I32, "w3_first")
+        nc.vector.tensor_copy(w3_first[:], w3_by_slice[:, :, 0])
+
+        mag0 = magnitudes(0)
+        sh0 = shifted(0)
+        neg = sb([P, PACK, 2, P * PACK], BF16, "w2_neg", "tab1")
+        for a in range(2):
+            nc.scalar.activation(
+                neg[:, :, a, :].rearrange("p t (m j) -> p m j t", j=PACK),
+                w2_raw[a][:].rearrange("p (j m t) -> p m j t", t=PACK, j=PACK),
+                ACT.Copy,
+                scale=-1.0,
+            )
+        neg_flat = neg[:].rearrange("p t a c -> p (t a c)")
+        mag_q = [quantise(mag0[:], "magq0")]
+        sh_q = [quantise(sh0[:], "shq0")]
+        w2_first = quantise(neg_flat[:, 0:1024], "w2q0")
+        mag1 = magnitudes(1)
+        sh1 = shifted(1)
+        sh_q.append(quantise(sh1[:], "shq1"))
+        mag_q.append(quantise(mag1[:], "magq1"))
+
+        w3_rest = sb([P, PACK - 1, 2 * P], I32, "w3_rest", "x1")
+        nc.vector.tensor_copy(w3_rest[:].rearrange("p t x -> p x t"), w3_by_slice[:, :, 1:PACK])
+        w2_second = quantise(neg_flat[:, 1024:2048], "w2q1", "mag1")
+        w2_last = quantise(neg_flat[:, 2048:4096], "w2q2", "sh1")
+        w2_q = [(w2_first, 0), (w2_second, 0), (w2_last, 0), (w2_last, 2 * P)]
+        w3_c = [w3_first[:], w3_rest[:, 0, :], w3_rest[:, 1, :], w3_rest[:, 2, :]]
+
+        out_rows = out.rearrange("(p i) t -> p i t", i=PACK)
+        for i in range(PACK):
+            bank = psum.tile([P, BANK], F32, name="bank")
+            (w2_codes, w2_plane), base = w2_q[i]
+
+            def w2_pass(a):
+                cols = slice(base + a * P, base + (a + 1) * P)
+                nc.tensor.matmul_mx(
+                    out=bank[:],
+                    lhsT=w2_codes[:, cols].bitcast(FP8X4),
+                    lhsT_scale=w2_plane[:, cols],
+                    rhs=sh_q[a][0][:].bitcast(FP8X4),
+                    rhs_scale=sh_q[a][1][:],
+                    start=False,
+                    stop=False,
+                )
+
+            def w3_pass(a):
+                nc.tensor.matmul_mx(
+                    out=bank[:],
+                    lhsT=w3_c[i][:, a * P : (a + 1) * P].bitcast(FP8X4),
+                    lhsT_scale=w3_sc[4 * a : P, i * P : (i + 1) * P],
+                    rhs=mag_q[a][0][:].bitcast(FP8X4),
+                    rhs_scale=mag_q[a][1][:],
+                    start=(a == 0),
+                    stop=(a == 1),
+                )
+
+            w3_pass(0)
+            w2_pass(0)
+            w2_pass(1)
+            w3_pass(1)
+            sq = sb([P, PICK], F32, f"sq{i}")
+            nc.scalar.activation(sq[:], bank[:], ACT.Square)
+            y = sb([P, PICK], F32, f"y{i}")
+            nc.scalar.activation(y[:], sq[:], ACT.Ln, bias=1.0)
+            nc.vector.tensor_tensor(pages[i][:].indirect(list3[:]), y[:], wgo_sb[:], ALU.mult)
+            nc.sync.dma_start(out_rows[:, i, :], pages[i][:])

@@ -28,7 +28,7 @@ def tile_list_pod_cure_deviation_kernel(
     nc = tc.nc
     with ExitStack() as ctx:
         keep = ctx.enter_context(tc.tile_pool(name="keep", bufs=1))
-        psum = ctx.enter_context(tc.psum_pool(name="psum", bufs=8))
+        psum = ctx.enter_context(tc.psum_pool(name="psum", bufs=1))
 
         def sb(shape, dtype, name, tag=""):
             return keep.tile(shape, dtype, name=name, tag=tag or name, align_bytes=64)
@@ -36,25 +36,23 @@ def tile_list_pod_cure_deviation_kernel(
         list1 = sb([P, S // 16], U16, "list1")
         list2 = sb([P, PICK // 16], U16, "list2")
         list3 = sb([P, PICK // 16], U16, "list3")
+        tab = [sb([P, T], I32, f"tab{a}") for a in range(2)]
         tab_sc = sb([P, T], U8, "tab_sc")
-        v_sc0 = sb([P, S], U8, "v_sc0")
-        v_sc1 = sb([P, S], U8, "v_sc1")
+        moved_sc = sb([P, S], U8, "moved_sc")
         w1_raw = [sb([P, 2 * H], U8, f"w1_raw{b}") for b in range(2)]
         w1_sc_raw = sb([P, 2 * H], U8, "w1_sc_raw")
         w3_sc_raw = sb([P, N], U8, "w3_sc_raw")
-        pages = [sb([P, T2], F32, f"page{i}") for i in range(PACK)]
         warm = sb([P, 1], F32, "warm")
         warm_out = sb([P, 1], F32, "warm_out")
 
-        nc.vector.memset(tab_sc[:].bitcast(I32), 0)
-        nc.vector.memset(w1_sc_raw[:].bitcast(I32), 0)
-        nc.vector.memset(warm[:], 1.0)
-        nc.vector.memset(v_sc1[:].bitcast(I32), 0)
-        for i in range(PACK):
-            nc.vector.memset(pages[i][:], 0.0)
-        nc.vector.memset(w3_sc_raw[:].bitcast(I32), 0)
+        def cleared_page(i, tag):
+            page = sb([P, T2], F32, f"page{i}", tag)
+            nc.gpsimd.memset(page[:], 0.0)
+            return page
 
-        tab = [sb([P, T], I32, f"tab{a}") for a in range(2)]
+        def load_table(a, half):
+            cols = slice(half * T // 2, (half + 1) * T // 2)
+            nc.sync.dma_start(tab[a][:, cols], tab_words[a].rearrange("p t i -> p (t i)").bitcast(I32)[:, cols])
 
         def load_w1(b):
             nc.sync.dma_start(
@@ -62,24 +60,34 @@ def tile_list_pod_cure_deviation_kernel(
                 w1_words[:, :, b * H : (b + 1) * H].bitcast(I32).rearrange("a p c -> p a c"),
             )
 
+        nc.gpsimd.memset(tab_sc[:].bitcast(I32), 0)
+        nc.gpsimd.memset(w1_sc_raw[:].bitcast(I32), 0)
+        nc.gpsimd.memset(warm[:], 1.0)
+        nc.gpsimd.memset(moved_sc[:].bitcast(I32), 0)
+        nc.gpsimd.memset(w3_sc_raw[:].bitcast(I32), 0)
+        nc.scalar.activation(warm_out[:], warm[:], ACT.Ln)
+        pages = [cleared_page(i, "") for i in range(PACK)]
+
         nc.sync.dma_start(list1[:], offs)
-        nc.sync.dma_start(tab[0][:], tab_words[0].rearrange("p t i -> p (t i)").bitcast(I32))
+        load_table(0, 0)
         for q in range(4):
-            nc.scalar.dma_start(
+            nc.sync.dma_start(
                 tab_sc[32 * q : 32 * q + 8, :].bitcast(I32), tab_scales[:, 4 * q : 4 * q + 4, :].bitcast(I32)
             )
+        load_table(0, 1)
+        load_w1(0)
         for q in range(4):
-            nc.scalar.dma_start(
+            nc.sync.dma_start(
                 w1_sc_raw[32 * q : 32 * q + 4, :].bitcast(I32).rearrange("r (a c) -> r a c", a=2),
                 w1_scales[:, 4 * q : 4 * q + 4, :].bitcast(I32).rearrange("a r c -> r a c"),
             )
-        load_w1(0)
-        nc.sync.dma_start(tab[1][:], tab_words[1].rearrange("p t i -> p (t i)").bitcast(I32))
-        nc.scalar.activation(warm_out[:], warm[:], ACT.Ln)
+        load_table(1, 0)
+        load_table(1, 1)
 
-        nc.vector.tensor_copy(v_sc0[:], tab_sc[:].indirect(list1[:]))
-        nc.scalar.dma_start(v_sc1[0 : P - 4, :].bitcast(I32), v_sc0[4:P, :].bitcast(I32))
-        v_sc = [v_sc0, v_sc1]
+        picked_sc = sb([P, S], U8, "picked_sc")
+        nc.vector.tensor_copy(picked_sc[:], tab_sc[:].indirect(list1[:]))
+        nc.scalar.dma_start(moved_sc[0 : P - 4, :].bitcast(I32), picked_sc[4:P, :].bitcast(I32))
+        v_sc = [picked_sc, moved_sc]
 
         load_w1(1)
         nc.sync.dma_start(list2[:], offs2)
@@ -117,24 +125,23 @@ def tile_list_pod_cure_deviation_kernel(
             )
             return dealt
 
-        v = [sb([P, S], U32, f"v{a}") for a in range(2)]
-        nc.vector.tensor_copy(v[0][:], tab[0][:].bitcast(U32).indirect(list1[:]))
+        v0 = sb([P, S], U32, "v0")
+        nc.vector.tensor_copy(v0[:], tab[0][:].bitcast(U32).indirect(list1[:]))
         w1 = [deal_w1(0, "")]
+        v1 = [sb([P, BANK], U32, f"v1_{j}") for j in range(2)]
         for j in range(2):
-            nc.vector.tensor_copy(
-                v[1][:, j * BANK : (j + 1) * BANK], tab[1][:].bitcast(U32).indirect(list1[:, 32 * j : 32 * (j + 1)])
-            )
+            nc.vector.tensor_copy(v1[j][:], tab[1][:].bitcast(U32).indirect(list1[:, 32 * j : 32 * (j + 1)]))
         w1.append(deal_w1(1, "tab1"))
+        v = [[v0[:, 0:BANK], v0[:, BANK:S]], [v1[0][:], v1[1][:]]]
 
         def stage1_pass(bank, a, b, t, j):
             c0 = a * KP + t * P
-            cols = slice(j * BANK, (j + 1) * BANK)
             nc.tensor.matmul_mx(
                 out=bank[:],
                 lhsT=w1[b][:, 2 * c0 : 2 * (c0 + P)].bitcast(FP4X4),
                 lhsT_scale=w1[b][:, 2 * H + c0 : 2 * H + c0 + P],
-                rhs=v[a][:, cols].bitcast(FP8X4),
-                rhs_scale=v_sc[a][:, cols],
+                rhs=v[a][j].bitcast(FP8X4),
+                rhs_scale=v_sc[a][:, j * BANK : (j + 1) * BANK],
                 start=(a == 0),
                 stop=(a == 1),
             )
@@ -156,49 +163,39 @@ def tile_list_pod_cure_deviation_kernel(
         def woven(tile):
             return tile[:].rearrange("p (c i t) -> p c t i", i=4, t=PACK)
 
-        def rows(b):
-            return x[b][:].rearrange("p t (c i) -> p c t i", i=4)
+        def rows(tile):
+            return tile[:].rearrange("p t (c i) -> p c t i", i=4)
 
-        def magnitudes(b):
-            mag = sb([P, PACK * PICK], BF16, f"mag{b}")
-            nc.scalar.activation(woven(mag), rows(b), ACT.Abs)
+        def magnitudes(b, tag):
+            mag = sb([P, PACK * PICK], BF16, f"mag{b}", tag)
+            nc.scalar.activation(woven(mag), rows(x[b]), ACT.Abs)
             return mag
 
-        def shifted(b):
-            sh = sb([P, PACK * PICK], BF16, f"sh{b}")
-            nc.vector.tensor_tensor(
-                woven(sh), rows(b), tgt[:, b, :].unsqueeze(1).unsqueeze(3).to_broadcast([P, PICK // 4, PACK, 4]), ALU.add
-            )
+        def shifted(b, tag):
+            sh = sb([P, PACK * PICK], BF16, f"sh{b}", tag)
+            per_row = tgt[:, b, :].unsqueeze(1).unsqueeze(3).to_broadcast([P, PICK // 4, PACK, 4])
+            nc.vector.tensor_tensor(woven(sh), rows(x[b]), per_row, ALU.add)
             return sh
 
-        first = [[psum.tile([P, BANK], F32, name="bank") for j in range(2)] for t in range(PACK)]
-        for t in range(PACK):
-            for j in range(2):
-                stage1_pass(first[t][j], 0, 0, t, j)
-        for j in range(2):
+        for b in range(2):
             for t in range(PACK):
-                stage1_pass(first[t][j], 1, 0, t, j)
-        for t in range(PACK):
-            pick(first[t], 0, t)
-        for t in range(PACK):
-            banks = [psum.tile([P, BANK], F32, name="bank") for j in range(2)]
-            for j in range(2):
-                for a in range(2):
-                    stage1_pass(banks[j], a, 1, t, j)
-            pick(banks, 1, t)
+                banks = [psum.tile([P, BANK], F32, name="h_bank", bufs=5) for j in range(2)]
+                for j in range(2):
+                    for a in range(2):
+                        stage1_pass(banks[j], a, b, t, j)
+                pick(banks, b, t)
 
-        w3_sc = sb([P, N], U8, "w3_sc")
+        w3_sc = sb([P, N], U8, "w3_sc", "h10")
         nc.vector.tensor_copy(
             w3_sc[:].rearrange("p (t m) -> p t m", t=PACK),
             w3_sc_raw[:].rearrange("p (m t) -> p t m", t=PACK),
         )
         w3_by_slice = w3_raw[:].rearrange("p (x t) -> p x t", t=PACK)
-        w3_first = sb([P, 2 * P], I32, "w3_first")
+        w3_first = sb([P, 2 * P], I32, "w3_first", "h11")
         nc.vector.tensor_copy(w3_first[:], w3_by_slice[:, :, 0])
 
-        mag0 = magnitudes(0)
-        sh0 = shifted(0)
-        neg = sb([P, PACK, 2, P * PACK], BF16, "w2_neg", "tab1")
+        sh_q = [quantise(shifted(0, "")[:], "shq0")]
+        neg = sb([P, PACK, 2, KP], BF16, "w2_neg", "tab1")
         for a in range(2):
             nc.scalar.activation(
                 neg[:, :, a, :].rearrange("p t (m j) -> p m j t", j=PACK),
@@ -207,56 +204,62 @@ def tile_list_pod_cure_deviation_kernel(
                 scale=-1.0,
             )
         neg_flat = neg[:].rearrange("p t a c -> p (t a c)")
+        w2_first = quantise(neg_flat[:, 0:H], "w2_first")
+        mag0 = magnitudes(0, "v1_1")
+        sh1 = shifted(1, "w2_raw1")
         mag_q = [quantise(mag0[:], "magq0")]
-        sh_q = [quantise(sh0[:], "shq0")]
-        w2_first = quantise(neg_flat[:, 0:1024], "w2q0")
-        mag1 = magnitudes(1)
-        sh1 = shifted(1)
         sh_q.append(quantise(sh1[:], "shq1"))
-        mag_q.append(quantise(mag1[:], "magq1"))
+        mag_q.append(quantise(magnitudes(1, "")[:], "magq1"))
 
         w3_rest = sb([P, PACK - 1, 2 * P], I32, "w3_rest", "x1")
         nc.vector.tensor_copy(w3_rest[:].rearrange("p t x -> p x t"), w3_by_slice[:, :, 1:PACK])
-        w2_second = quantise(neg_flat[:, 1024:2048], "w2q1", "mag1")
-        w2_last = quantise(neg_flat[:, 2048:4096], "w2q2", "sh1")
-        w2_q = [(w2_first, 0), (w2_second, 0), (w2_last, 0), (w2_last, 2 * P)]
+        rest_codes = sb([P, 3 * 2 * P], U32, "w2_rest_c", "mag1")
+        rest_plane = sb([P, 3 * 2 * P], U8, "w2_rest_s")
+        for c0, c1 in ((0, 2 * P), (2 * P, 6 * P)):
+            nc.vector.quantize_mx(
+                out=rest_codes[:, c0:c1].bitcast(FP8X4),
+                scales=rest_plane[:, c0:c1],
+                in_=neg_flat[:, H + PACK * c0 : H + PACK * c1],
+            )
         w3_c = [w3_first[:], w3_rest[:, 0, :], w3_rest[:, 1, :], w3_rest[:, 2, :]]
 
-        out_rows = out.rearrange("(p i) t -> p i t", i=PACK)
-        for i in range(PACK):
-            bank = psum.tile([P, BANK], F32, name="bank")
-            (w2_codes, w2_plane), base = w2_q[i]
+        def w2_operand(i, a):
+            (codes, plane), c = (w2_first, a) if i == 0 else ((rest_codes, rest_plane), 2 * (i - 1) + a)
+            return codes[:, c * P : (c + 1) * P], plane[:, c * P : (c + 1) * P]
 
-            def w2_pass(a):
-                cols = slice(base + a * P, base + (a + 1) * P)
+        def w3_operand(i, a):
+            return w3_c[i][:, a * P : (a + 1) * P], w3_sc[4 * a : P, i * P : (i + 1) * P]
+
+        def scores(i, cols, name):
+            width = cols.stop - cols.start
+            bank = psum.tile([P, BANK], F32, name="y_bank", bufs=3)
+            passes = [
+                (w2_operand(i, 0), sh_q[0]),
+                (w3_operand(i, 0), mag_q[0]),
+                (w2_operand(i, 1), sh_q[1]),
+                (w3_operand(i, 1), mag_q[1]),
+            ]
+            for n, ((w_codes, w_plane), (codes, plane)) in enumerate(passes):
                 nc.tensor.matmul_mx(
-                    out=bank[:],
-                    lhsT=w2_codes[:, cols].bitcast(FP8X4),
-                    lhsT_scale=w2_plane[:, cols],
-                    rhs=sh_q[a][0][:].bitcast(FP8X4),
-                    rhs_scale=sh_q[a][1][:],
-                    start=False,
-                    stop=False,
+                    out=bank[:, 0:width],
+                    lhsT=w_codes.bitcast(FP8X4),
+                    lhsT_scale=w_plane,
+                    rhs=codes[:, cols].bitcast(FP8X4),
+                    rhs_scale=plane[:, cols],
+                    start=(n == 0),
+                    stop=(n == len(passes) - 1),
                 )
-
-            def w3_pass(a):
-                nc.tensor.matmul_mx(
-                    out=bank[:],
-                    lhsT=w3_c[i][:, a * P : (a + 1) * P].bitcast(FP8X4),
-                    lhsT_scale=w3_sc[4 * a : P, i * P : (i + 1) * P],
-                    rhs=mag_q[a][0][:].bitcast(FP8X4),
-                    rhs_scale=mag_q[a][1][:],
-                    start=(a == 0),
-                    stop=(a == 1),
-                )
-
-            w3_pass(0)
-            w2_pass(0)
-            w2_pass(1)
-            w3_pass(1)
-            sq = sb([P, PICK], F32, f"sq{i}")
-            nc.scalar.activation(sq[:], bank[:], ACT.Square)
-            y = sb([P, PICK], F32, f"y{i}")
+            sq = sb([P, width], F32, "sq" + name)
+            nc.scalar.activation(sq[:], bank[:, 0:width], ACT.Square)
+            y = sb([P, width], F32, "y" + name)
             nc.scalar.activation(y[:], sq[:], ACT.Ln, bias=1.0)
-            nc.vector.tensor_tensor(pages[i][:].indirect(list3[:]), y[:], wgo_sb[:], ALU.mult)
+            offsets = list3[:, cols.start // 16 : cols.stop // 16]
+            nc.vector.tensor_tensor(pages[i][:].indirect(offsets), y[:], wgo_sb[:, cols], ALU.mult)
+
+        out_rows = out.rearrange("(p i) t -> p i t", i=PACK)
+        scores(0, slice(0, PICK // 2), "0a")
+        scores(0, slice(PICK // 2, PICK), "0b")
+        nc.sync.dma_start(out_rows[:, 0, :], pages[0][:])
+        for i in range(1, PACK):
+            scores(i, slice(0, PICK), str(i))
             nc.sync.dma_start(out_rows[:, i, :], pages[i][:])

@@ -70,9 +70,10 @@ def tile_list_pod_cure_deviation_kernel(
 
         nc.sync.dma_start(list1[:], offs)
         load_table(0, 0)
-        for q in range(4):
+        for r in range(4):
             nc.sync.dma_start(
-                tab_sc[32 * q : 32 * q + 8, :].bitcast(I32), tab_scales[:, 4 * q : 4 * q + 4, :].bitcast(I32)
+                tab_sc[r:P:16, :].bitcast(I32),
+                tab_scales.bitcast(I32).rearrange("a (q r) t -> r q a t", r=4)[r],
             )
         load_table(0, 1)
         load_w1(0)
@@ -86,7 +87,7 @@ def tile_list_pod_cure_deviation_kernel(
 
         picked_sc = sb([P, S], U8, "picked_sc")
         nc.vector.tensor_copy(picked_sc[:], tab_sc[:].indirect(list1[:]))
-        nc.scalar.dma_start(moved_sc[0 : P - 4, :].bitcast(I32), picked_sc[4:P, :].bitcast(I32))
+        nc.scalar.dma_start(moved_sc[0 : P - 16, :].bitcast(I32), picked_sc[16:P, :].bitcast(I32))
         v_sc = [picked_sc, moved_sc]
 
         load_w1(1)
@@ -161,10 +162,10 @@ def tile_list_pod_cure_deviation_kernel(
             return codes, plane
 
         def woven(tile):
-            return tile[:].rearrange("p (c i t) -> p c t i", i=4, t=PACK)
+            return tile[:].rearrange("p (c i t) -> p c t i", i=2, t=PACK)
 
         def rows(tile):
-            return tile[:].rearrange("p t (c i) -> p c t i", i=4)
+            return tile[:].rearrange("p t (c i) -> p c t i", i=2)
 
         def magnitudes(b, tag):
             mag = sb([P, PACK * PICK], BF16, f"mag{b}", tag)
@@ -173,7 +174,7 @@ def tile_list_pod_cure_deviation_kernel(
 
         def shifted(b, tag):
             sh = sb([P, PACK * PICK], BF16, f"sh{b}", tag)
-            per_row = tgt[:, b, :].unsqueeze(1).unsqueeze(3).to_broadcast([P, PICK // 4, PACK, 4])
+            per_row = tgt[:, b, :].unsqueeze(1).unsqueeze(3).to_broadcast([P, PICK // 2, PACK, 2])
             nc.vector.tensor_tensor(woven(sh), rows(x[b]), per_row, ALU.add)
             return sh
 

from contextlib import ExitStack

import concourse.mybir as mybir

K, H, N, T, S, PICK, T2 = 1024, 1024, 512, 4096, 1024, 512, 1024
FLOPS = 2 * K * H * S + 2 * 2 * H * N * PICK

F32 = mybir.dt.float32
BF16 = mybir.dt.bfloat16
I32 = mybir.dt.int32
U32 = mybir.dt.uint32
U16 = mybir.dt.uint16
U8 = mybir.dt.uint8
FP8X4 = mybir.dt.float8_e4m3fn_x4
FP4X4 = mybir.dt.float4_e2m1fn_x4
ACT = mybir.ActivationFunctionType
ALU = mybir.AluOpType

P = 128
PACK = 4
KP = P * PACK
BANK = 512


def tile_list_pod_cure_deviation_kernel(
    tc, tab_words, tab_scales, offs, w1_words, w1_scales, offs2, wgt, target, w2, w3_words, w3_scales, offs3, wgo, out
):
    nc = tc.nc
    with ExitStack() as ctx:
        keep = ctx.enter_context(tc.tile_pool(name="keep", bufs=1))
        psum = ctx.enter_context(tc.psum_pool(name="psum", bufs=1))

        def sb(shape, dtype, name, tag=""):
            return keep.tile(shape, dtype, name=name, tag=tag or name, align_bytes=64)

        list1 = sb([P, S // 16], U16, "list1")
        list2 = sb([P, PICK // 16], U16, "list2")
        list3 = sb([P, PICK // 16], U16, "list3")
        tab = [sb([P, T], I32, f"tab{a}") for a in range(2)]
        tab_sc = sb([P, T], U8, "tab_sc")
        moved_sc = sb([P, S], U8, "moved_sc")
        w1_raw = [sb([P, 2 * H], U8, f"w1_raw{b}") for b in range(2)]
        w1_sc_raw = sb([P, 2 * H], U8, "w1_sc_raw")
        w3_sc_raw = sb([P, N], U8, "w3_sc_raw")
        warm = sb([P, 1], F32, "warm")
        warm_out = sb([P, 1], F32, "warm_out")

        def cleared_page(i, tag):
            page = sb([P, T2], F32, f"page{i}", tag)
            nc.gpsimd.memset(page[:], 0.0)
            return page

        def load_table(a, half):
            cols = slice(half * T // 2, (half + 1) * T // 2)
            nc.sync.dma_start(tab[a][:, cols], tab_words[a].rearrange("p t i -> p (t i)").bitcast(I32)[:, cols])

        def load_w1(b):
            nc.sync.dma_start(
                w1_raw[b][:].bitcast(I32).rearrange("p (a c) -> p a c", a=2),
                w1_words[:, :, b * H : (b + 1) * H].bitcast(I32).rearrange("a p c -> p a c"),
            )

        nc.gpsimd.memset(tab_sc[:].bitcast(I32), 0)
        nc.gpsimd.memset(w1_sc_raw[:].bitcast(I32), 0)
        nc.gpsimd.memset(warm[:], 1.0)
        nc.gpsimd.memset(moved_sc[:].bitcast(I32), 0)
        nc.gpsimd.memset(w3_sc_raw[:].bitcast(I32), 0)
        nc.scalar.activation(warm_out[:], warm[:], ACT.Ln)
        pages = [cleared_page(i, "") for i in range(PACK)]

        nc.sync.dma_start(list1[:], offs)
        load_table(0, 0)
        for r in range(4):
            nc.sync.dma_start(
                tab_sc[r:P:16, :].bitcast(I32),
                tab_scales.bitcast(I32).rearrange("a (q r) t -> r q a t", r=4)[r],
            )
        load_table(0, 1)
        load_w1(0)
        for q in range(4):
            nc.sync.dma_start(
                w1_sc_raw[32 * q : 32 * q + 4, :].bitcast(I32).rearrange("r (a c) -> r a c", a=2),
                w1_scales[:, 4 * q : 4 * q + 4, :].bitcast(I32).rearrange("a r c -> r a c"),
            )
        load_table(1, 0)
        load_table(1, 1)

        picked_sc = sb([P, S], U8, "picked_sc")
        nc.vector.tensor_copy(picked_sc[:], tab_sc[:].indirect(list1[:]))
        nc.scalar.dma_start(moved_sc[0 : P - 16, :].bitcast(I32), picked_sc[16:P, :].bitcast(I32))
        v_sc = [picked_sc, moved_sc]

        load_w1(1)
        nc.sync.dma_start(list2[:], offs2)
        wgt_sb = sb([P, PICK], F32, "wgt_sb")
        nc.sync.dma_start(wgt_sb[:], wgt)
        tgt = sb([P, 2, PACK], F32, "tgt")
        nc.sync.dma_start(tgt[:], target.rearrange("(b p t) -> p b t", b=2, t=PACK))
        w2_raw = []
        for a in range(2):
            raw = sb([P, PACK * N], F32, f"w2_raw{a}")
            nc.sync.dma_start(raw[:], w2[a * KP : (a + 1) * KP, :].rearrange("(p j) n -> p (j n)", j=PACK))
            w2_raw.append(raw)
        w3_raw = sb([P, 2 * N], I32, "w3_raw")
        nc.sync.dma_start(
            w3_raw[:].rearrange("p (a c) -> p a c", a=2),
            w3_words.rearrange("a p c i -> p a (c i)").bitcast(I32),
        )
        for q in range(4):
            nc.sync.dma_start(
                w3_sc_raw[32 * q : 32 * q + 8, :].bitcast(I32), w3_scales[:, 4 * q : 4 * q + 4, :].bitcast(I32)
            )
        nc.sync.dma_start(list3[:], offs3)
        wgo_sb = sb([P, PICK], F32, "wgo_sb")
        nc.sync.dma_start(wgo_sb[:], wgo)

        def deal_w1(b, tag):
            dealt = sb([P, 3 * H], U8, f"w1_dealt{b}", tag)
            nc.vector.tensor_copy(
                dealt[:, 0 : 2 * H].bitcast(U16).rearrange("p (a t m) -> p a t m", t=PACK, m=P),
                w1_raw[b][:].bitcast(U16).rearrange("p (a m t) -> p a t m", t=PACK, m=P),
            )
            nc.vector.tensor_copy(
                dealt[:, 2 * H : 3 * H].rearrange("p (a t m) -> p a t m", t=PACK, m=P),
                w1_sc_raw[:].rearrange("p (a b m t) -> p b a t m", a=2, t=PACK, m=P)[:, b],
            )
            return dealt

        v0 = sb([P, S], U32, "v0")
        nc.vector.tensor_copy(v0[:], tab[0][:].bitcast(U32).indirect(list1[:]))
        w1 = [deal_w1(0, "")]
        v1 = [sb([P, BANK], U32, f"v1_{j}") for j in range(2)]
        for j in range(2):
            nc.vector.tensor_copy(v1[j][:], tab[1][:].bitcast(U32).indirect(list1[:, 32 * j : 32 * (j + 1)]))
        w1.append(deal_w1(1, "tab1"))
        v = [[v0[:, 0:BANK], v0[:, BANK:S]], [v1[0][:], v1[1][:]]]

        def stage1_pass(bank, a, b, t, j):
            c0 = a * KP + t * P
            nc.tensor.matmul_mx(
                out=bank[:],
                lhsT=w1[b][:, 2 * c0 : 2 * (c0 + P)].bitcast(FP4X4),
                lhsT_scale=w1[b][:, 2 * H + c0 : 2 * H + c0 + P],
                rhs=v[a][j].bitcast(FP8X4),
                rhs_scale=v_sc[a][:, j * BANK : (j + 1) * BANK],
                start=(a == 0),
                stop=(a == 1),
            )

        x = [sb([P, PACK, PICK], F32, f"x{b}") for b in range(2)]

        def pick(banks, b, t):
            h = sb([P, S], F32, f"h{b}{t}")
            for j in range(2):
                nc.scalar.copy(h[:, j * BANK : (j + 1) * BANK], banks[j][:])
            nc.vector.tensor_tensor(x[b][:, t, :], h[:].indirect(list2[:]), wgt_sb[:], ALU.mult)

        def quantise(src, name, tag=""):
            codes = sb([P, src.shape[1] // PACK], U32, name + "_c", tag)
            plane = sb([P, src.shape[1] // PACK], U8, name + "_s")
            nc.vector.quantize_mx(out=codes[:].bitcast(FP8X4), scales=plane[:], in_=src)
            return codes, plane

        def woven(tile):
            return tile[:].rearrange("p (c i t) -> p c t i", i=2, t=PACK)

        def rows(tile):
            return tile[:].rearrange("p t (c i) -> p c t i", i=2)

        def magnitudes(b, tag):
            mag = sb([P, PACK * PICK], BF16, f"mag{b}", tag)
            nc.scalar.activation(woven(mag), rows(x[b]), ACT.Abs)
            return mag

        def shifted(b, tag):
            sh = sb([P, PACK * PICK], BF16, f"sh{b}", tag)
            per_row = tgt[:, b, :].unsqueeze(1).unsqueeze(3).to_broadcast([P, PICK // 2, PACK, 2])
            nc.vector.tensor_tensor(woven(sh), rows(x[b]), per_row, ALU.add)
            return sh

        for b in range(2):
            for t in range(PACK):
                banks = [psum.tile([P, BANK], F32, name="h_bank", bufs=5) for j in range(2)]
                for j in range(2):
                    for a in range(2):
                        stage1_pass(banks[j], a, b, t, j)
                pick(banks, b, t)

        w3_sc = sb([P, N], U8, "w3_sc", "h10")
        nc.vector.tensor_copy(
            w3_sc[:].rearrange("p (t m) -> p t m", t=PACK),
            w3_sc_raw[:].rearrange("p (m t) -> p t m", t=PACK),
        )
        w3_by_slice = w3_raw[:].rearrange("p (x t) -> p x t", t=PACK)
        w3_first = sb([P, 2 * P], I32, "w3_first", "h11")
        nc.vector.tensor_copy(w3_first[:], w3_by_slice[:, :, 0])

        sh_q = [quantise(shifted(0, "")[:], "shq0")]
        neg = sb([P, PACK, 2, KP], BF16, "w2_neg", "tab1")
        for a in range(2):
            nc.scalar.activation(
                neg[:, :, a, :].rearrange("p t (m j) -> p m j t", j=PACK),
                w2_raw[a][:].rearrange("p (j m t) -> p m j t", t=PACK, j=PACK),
                ACT.Copy,
                scale=-1.0,
            )
        neg_flat = neg[:].rearrange("p t a c -> p (t a c)")
        w2_first = quantise(neg_flat[:, 0:H], "w2_first")
        mag0 = magnitudes(0, "v1_1")
        sh1 = shifted(1, "w2_raw1")
        mag_q = [quantise(mag0[:], "magq0")]
        sh_q.append(quantise(sh1[:], "shq1"))
        mag_q.append(quantise(magnitudes(1, "")[:], "magq1"))

        w3_rest = sb([P, PACK - 1, 2 * P], I32, "w3_rest", "x1")
        nc.vector.tensor_copy(w3_rest[:].rearrange("p t x -> p x t"), w3_by_slice[:, :, 1:PACK])
        rest_codes = sb([P, 3 * 2 * P], U32, "w2_rest_c", "mag1")
        rest_plane = sb([P, 3 * 2 * P], U8, "w2_rest_s")
        for c0, c1 in ((0, 2 * P), (2 * P, 6 * P)):
            nc.vector.quantize_mx(
                out=rest_codes[:, c0:c1].bitcast(FP8X4),
                scales=rest_plane[:, c0:c1],
                in_=neg_flat[:, H + PACK * c0 : H + PACK * c1],
            )
        w3_c = [w3_first[:], w3_rest[:, 0, :], w3_rest[:, 1, :], w3_rest[:, 2, :]]

        def w2_operand(i, a):
            (codes, plane), c = (w2_first, a) if i == 0 else ((rest_codes, rest_plane), 2 * (i - 1) + a)
            return codes[:, c * P : (c + 1) * P], plane[:, c * P : (c + 1) * P]

        def w3_operand(i, a):
            return w3_c[i][:, a * P : (a + 1) * P], w3_sc[4 * a : P, i * P : (i + 1) * P]

        def scores(i, cols, name):
            width = cols.stop - cols.start
            bank = psum.tile([P, BANK], F32, name="y_bank", bufs=3)
            passes = [
                (w2_operand(i, 0), sh_q[0]),
                (w3_operand(i, 0), mag_q[0]),
                (w2_operand(i, 1), sh_q[1]),
                (w3_operand(i, 1), mag_q[1]),
            ]
            for n, ((w_codes, w_plane), (codes, plane)) in enumerate(passes):
                nc.tensor.matmul_mx(
                    out=bank[:, 0:width],
                    lhsT=w_codes.bitcast(FP8X4),
                    lhsT_scale=w_plane,
                    rhs=codes[:, cols].bitcast(FP8X4),
                    rhs_scale=plane[:, cols],
                    start=(n == 0),
                    stop=(n == len(passes) - 1),
                )
            sq = sb([P, width], F32, "sq" + name)
            nc.scalar.activation(sq[:], bank[:, 0:width], ACT.Square)
            y = sb([P, width], F32, "y" + name)
            nc.scalar.activation(y[:], sq[:], ACT.Ln, bias=1.0)
            offsets = list3[:, cols.start // 16 : cols.stop // 16]
            nc.vector.tensor_tensor(pages[i][:].indirect(offsets), y[:], wgo_sb[:, cols], ALU.mult)

        out_rows = out.rearrange("(p i) t -> p i t", i=PACK)
        scores(0, slice(0, PICK // 2), "0a")
        scores(0, slice(PICK // 2, PICK), "0b")
        nc.sync.dma_start(out_rows[:, 0, :], pages[0][:])
        for i in range(1, PACK):
            scores(i, slice(0, PICK), str(i))
            nc.sync.dma_start(out_rows[:, i, :], pages[i][:])
